import numpy as np
import ml_dtypes


def mxq(x, axis, fmt="e4m3"):
    dtype, down = {"e4m3": (ml_dtypes.float8_e4m3fn, 7), "e5m2": (ml_dtypes.float8_e5m2, 14)}[fmt]
    v = np.moveaxis(np.asarray(x, np.float32).astype(ml_dtypes.bfloat16).astype(np.float64), axis, -1)
    blocks = v.reshape(v.shape[:-1] + (-1, 32))
    amax = np.abs(blocks).max(-1, keepdims=True)
    byte = np.maximum(np.where(amax > 0, np.frexp(amax)[1] - 1 + 127, 0) - down, 1)
    scale = np.exp2(byte - 127.0)
    codes = (blocks / scale).astype(np.float32).astype(dtype).astype(np.float64)
    return np.moveaxis((codes * scale).reshape(v.shape), -1, axis)


WIDE = False


def mx_kscale(k):
    if not WIDE:
        return np.ones(k)
    levels = np.array([10, -10, 5, -5, 0])
    if k % 512:
        return np.exp2(np.random.permutation(np.resize(levels, k // 32))).repeat(32)
    a = np.empty((k // 512, 16))
    for p in range(k // 512):
        a[p, :8] = np.random.permutation(np.resize(levels, 8))
        for g in range(8):
            far = levels[np.abs(levels - a[p, g]) >= 10]
            a[p, g + 8] = far[np.random.randint(len(far))]
    return np.exp2(a.ravel()).repeat(32)


def f64(x):
    return np.asarray(x).astype(np.float64)


def striped(idx):
    return np.tile(idx.reshape(-1, 16).T, (8, 1)).astype(np.uint16)


def unstriped(offs):
    return offs[:16].T.reshape(-1).astype(np.int64)


def striped8(idx):
    return np.concatenate([x.reshape(-1, 16).T for x in idx]).astype(np.uint16)


def runs(offs, k):
    lists = np.stack([offs[16 * r : 16 * r + 16].T.reshape(-1) for r in range(8)]).astype(np.int64)
    return lists[np.arange(k) % 512 // 64]


def pack_weight(w):
    k, n = w.shape
    w = f64(np.asarray(w, np.float32).astype(ml_dtypes.bfloat16)).reshape(k // 32, 32, n)
    amax = np.abs(w).max(1)
    byte = np.clip(np.where(amax > 0, np.frexp(amax)[1] - 1 + 127 - 7, 1), 1, 254)
    scaled = (w * np.exp2(127.0 - byte)[:, None, :]).reshape(k, n).astype(np.float32)
    words = np.ascontiguousarray(scaled.reshape(k // 512, 128, 4, n).transpose(0, 1, 3, 2)).astype(ml_dtypes.float8_e4m3fn).view(np.uint8)
    return words, np.ascontiguousarray(byte.astype(np.uint8).reshape(k // 512, 16, n))


def unpack_weight(words, scales):
    g, p, n, _ = words.shape
    vals = np.ascontiguousarray(words).view(ml_dtypes.float8_e4m3fn).astype(np.float64) * np.repeat(np.exp2(scales.astype(np.float64) - 127.0), 8, axis=1)[..., None]
    return vals.transpose(0, 1, 3, 2).reshape(g * 512, n)


def sigmoid(v):
    return 1.0 / (1.0 + np.exp(-np.maximum(v, -700.0)))

def planes(y):
    n, m = y.shape
    v = y.astype(np.float32).astype(ml_dtypes.bfloat16).astype(np.float64).reshape(n // 32, 32, m)
    top = np.abs(v).max(1)
    byte = np.clip(np.where(top > 0, np.frexp(top)[1] - 1 + 127 - 7, 1), 1, 254)
    codes = (v * np.exp2(127.0 - byte)[:, None, :]).reshape(n, m).astype(np.float32).astype(ml_dtypes.float8_e4m3fn).view(np.uint8)
    words = codes.reshape(n // 512, 128, 4, m).transpose(0, 1, 3, 2)
    return np.ascontiguousarray(words), np.ascontiguousarray(byte.astype(np.uint8).reshape(n // 512, 16, m))


K, T, S, H, W = 512, 2048, 512, 512, 256


def setup_inputs():
    n = np.random.standard_normal
    s = mx_kscale(K)[:, None]
    u = mx_kscale(H)
    packed_xT = pack_weight(n((K, T)) * s)
    packed_w1 = pack_weight(n((K, H)) / np.sqrt(K) / s)
    packed_w2 = pack_weight(n((H, H)) / np.sqrt(H) / u[:, None])
    perm = np.stack([np.random.permutation(S) for _ in range(8)])
    perm2 = np.stack([np.random.permutation(S) for _ in range(8)])
    return {
        "x_words": packed_xT[0],
        "x_scales": packed_xT[1],
        "w1_words": packed_w1[0],
        "w1_scales": packed_w1[1],
        "gn": (np.random.uniform(0.5, 1.5, (H, 1)) * u[:, None]).astype(np.float32),
        "w2_words": packed_w2[0],
        "w2_scales": packed_w2[1],
        "offs": striped(np.random.permutation(T)[:S]),
        "n1": striped8(perm[:, :W]),
        "n2": striped8(perm[:, W:]),
        "n3": striped8(perm2[:, :W]),
        "n4": striped8(perm2[:, W:]),
        "n5": striped(np.random.permutation(S)),
        "n6": striped(np.random.permutation(S)),
        "n7": striped(np.random.permutation(S)),
        "n8": striped(np.random.permutation(S)),
    }


def reference(x_words, x_scales, w1_words, w1_scales, gn, w2_words, w2_scales, offs, n1, n2, n3, n4, n5, n6, n7, n8):
    xq = unpack_weight(x_words, x_scales)[:, unstriped(offs)]
    y = unpack_weight(w1_words, w1_scales).T @ xq
    pa = y[np.arange(H)[:, None], runs(n1, H)]
    pb = y[np.arange(H)[:, None], runs(n2, H)]
    rb = np.minimum(pa, pb)
    ra = np.maximum(pa, pb)
    ds = np.zeros((H, S))
    ds[np.arange(H)[:, None], runs(n1, H)] = ra
    dt = ds.copy()
    dt[np.arange(H)[:, None], runs(n2, H)] = rb
    z = f64(gn) * dt
    w2q = unpack_weight(w2_words, w2_scales)
    a = w2q.T @ mxq(z, 0, "e4m3")
    pb2 = y[np.arange(H)[:, None], runs(n4, H)]
    pa2 = y[np.arange(H)[:, None], runs(n3, H)]
    rb2 = pb2 * sigmoid(pb2 - pa2)
    ra2 = pa2 * sigmoid(pa2 - pb2)
    ds2 = np.zeros((H, S))
    ds2[np.arange(H)[:, None], runs(n3, H)] = ra2
    dt2 = ds2.copy()
    dt2[np.arange(H)[:, None], runs(n4, H)] = rb2
    z2 = f64(gn) * dt2
    b = w2q.T @ mxq(z2, 0, "e4m3")
    out_0 = np.maximum(a[:, unstriped(n5)] + b[:, unstriped(n7)], a[:, unstriped(n6)] + b[:, unstriped(n8)])
    return (out_0,) + planes(out_0)

@@ -1,0 +1,274 @@
+from contextlib import ExitStack
+
+import concourse.mybir as mybir
+
+F32 = mybir.dt.float32
+BF16 = mybir.dt.bfloat16
+I32 = mybir.dt.int32
+U32 = mybir.dt.uint32
+U16 = mybir.dt.uint16
+U8 = mybir.dt.uint8
+FP8X4 = mybir.dt.float8_e4m3fn_x4
+ALU = mybir.AluOpType
+ACT = mybir.ActivationFunctionType
+
+P = 128
+PACK = 4
+T = 2048
+S = 512
+W = 256
+HALF = S // 2
+FLOPS = 3 * 2 * 512 * 512 * 512
+
+
+def tile_picked_tiepathborderduel_none_po_kernel(
+    tc, x_words, x_scales, w1_words, w1_scales, gn, w2_words, w2_scales,
+    offs, n1, n2, n3, n4, n5, n6, n7, n8, out_0, out_1, out_2,
+):
+    nc = tc.nc
+    with ExitStack() as ctx:
+        lists = ctx.enter_context(tc.tile_pool(name="lists", bufs=1))
+        keep = ctx.enter_context(tc.tile_pool(name="keep", bufs=1))
+        psum = ctx.enter_context(tc.psum_pool(name="psum", bufs=8))
+
+        def sb(name, shape, dtype, tag=None):
+            return keep.tile(shape, dtype, name=name, tag=tag or name, align_bytes=64)
+
+        def load_list(name, src):
+            tile = lists.tile(list(src.shape), U16, name=name)
+            nc.sync.dma_start(tile[:], src)
+            return tile
+
+        def half_of(lst, h):
+            return lst[:, h * (HALF // 16):(h + 1) * (HALF // 16)]
+
+        def cols(h):
+            return slice(h * HALF, (h + 1) * HALF)
+
+        def words_of(src):
+            return src[0].rearrange("p n t -> p (n t)").bitcast(I32)
+
+        def load_scale_rows(queue, plane, src, q):
+            queue.dma_start(plane[32 * q:32 * q + 4, :].bitcast(I32), src[0, 4 * q:4 * q + 4, :].bitcast(I32))
+
+        def dealt(ap):
+            return ap.rearrange("p (m t) -> p t m", t=PACK)
+
+        def product(name, ww, ws, t, words, plane):
+            acc = psum.tile([P, words.shape[1]], F32, name=name, tag="acc")
+            nc.tensor.matmul_mx(out=acc[:], lhsT=ww[:, t, :].bitcast(FP8X4), lhsT_scale=ws[:, t, :],
+                                rhs=words.bitcast(FP8X4), rhs_scale=plane, start=True, stop=True)
+            return acc
+
+        def gather_s(out, window, lst):
+            nc.scalar.activation(out, window[:].indirect(lst), ACT.Copy)
+
+        def weave(engine_copy, dst, src):
+            engine_copy(dst.rearrange("p (c i) t -> p c t i", i=4), src.rearrange("p t (c i) -> p c t i", i=4))
+
+        xs = sb("xs", [P, T], U8)
+        w1s_raw = sb("w1s_raw", [P, S], U8)
+        w2s_raw = sb("w2s_raw", [P, S], U8)
+        nc.gpsimd.memset(xs[:].bitcast(I32), 0)
+        nc.vector.memset(w1s_raw[:].bitcast(I32), 0)
+        nc.vector.memset(w2s_raw[:].bitcast(I32), 0)
+        l_offs = load_list("l_offs", offs)
+        l1 = load_list("l1", n1)
+        l2 = load_list("l2", n2)
+        xw = sb("xw", [P, T], U32)
+        nc.sync.dma_start(xw[:].bitcast(I32), words_of(x_words))
+        for q in range(4):
+            load_scale_rows(nc.scalar, xs, x_scales, q)
+        w1w_raw = sb("w1w_raw", [P, S], I32)
+        nc.sync.dma_start(w1w_raw[:], words_of(w1_words))
+        for q in range(4):
+            load_scale_rows(nc.scalar if q < 2 else nc.gpsimd, w1s_raw, w1_scales, q)
+        w2w_raw = sb("w2w_raw", [P, S], I32)
+        nc.sync.dma_start(w2w_raw[:], words_of(w2_words))
+        l3 = load_list("l3", n3)
+        l4 = load_list("l4", n4)
+        gain = sb("gain", [P, PACK], F32)
+        nc.sync.dma_start(gain[:], gn.rearrange("(p t) o -> p (t o)", t=PACK))
+        for q in range(4):
+            load_scale_rows(nc.sync, w2s_raw, w2_scales, q)
+        l5 = load_list("l5", n5)
+        l6 = load_list("l6", n6)
+        l7 = load_list("l7", n7)
+        l8 = load_list("l8", n8)
+
+        xgs = sb("xgs", [P, S], U8)
+        xg = sb("xg", [P, S], U32)
+        w1s = sb("w1s", [P, PACK, P], U8)
+        w1w = sb("w1w", [P, PACK, P], I32)
+        nc.vector.tensor_copy(xgs[:], xs[:].indirect(l_offs[:]))
+        nc.vector.tensor_copy(xg[:, cols(0)], xw[:].indirect(half_of(l_offs, 0)))
+        nc.vector.tensor_copy(w1w[:, 0, :], dealt(w1w_raw[:])[:, 0, :])
+        nc.vector.tensor_copy(w1s[:], dealt(w1s_raw[:]))
+        nc.vector.tensor_copy(xg[:, cols(1)], xw[:].indirect(half_of(l_offs, 1)))
+        nc.vector.tensor_copy(w1w[:, 1:, :], dealt(w1w_raw[:])[:, 1:, :])
+
+        y = [sb("y%d" % t, [P, S], F32) for t in range(PACK)]
+        first = [product("y0_%d" % h, w1w, w1s, 0, xg[:, cols(h)], xgs[:, cols(h)]) for h in range(2)]
+        yacc = [None] + [product("yacc%d" % t, w1w, w1s, t, xg[:], xgs[:]) for t in range(1, PACK)]
+
+        w2s = sb("w2s", [P, PACK, P], U8)
+        w2w = sb("w2w", [P, PACK, P], I32)
+
+        pa = sb("pa", [P, PACK, W], F32)
+        pb = sb("pb", [P, PACK, W], F32)
+        ra = sb("ra", [P, PACK, W], F32)
+        rb = sb("rb", [P, PACK, W], F32)
+        pa2 = sb("pa2", [P, PACK, W], F32)
+        pb2 = sb("pb2", [P, PACK, W], F32)
+        diff = sb("diff", [P, PACK, W], F32)
+        sp = sb("sp", [P, PACK, W], F32)
+        sn = sb("sn", [P, PACK, W], F32)
+        dt = [sb("dt%d" % t, [P, S], F32) for t in range(PACK)]
+
+        def order_pairs(t0, t1):
+            nc.vector.tensor_tensor(ra[:, t0:t1, :], pa[:, t0:t1, :], pb[:, t0:t1, :], ALU.max)
+            nc.vector.tensor_tensor(rb[:, t0:t1, :], pa[:, t0:t1, :], pb[:, t0:t1, :], ALU.min)
+            for t in range(t0, t1):
+                nc.vector.tensor_copy(dt[t][:].indirect(l1[:]), ra[:, t, :])
+            for t in range(t0, t1):
+                nc.vector.tensor_copy(dt[t][:].indirect(l2[:]), rb[:, t, :])
+
+        def fetch_a(t):
+            gather_s(pa[:, t, :], y[t], l1[:])
+            gather_s(pb[:, t, :], y[t], l2[:])
+
+        def fetch_b(t):
+            gather_s(pa2[:, t, :], y[t], l3[:])
+            gather_s(pb2[:, t, :], y[t], l4[:])
+
+        def difference(t0, t1):
+            nc.vector.tensor_tensor(diff[:, t0:t1, :], pa2[:, t0:t1, :], pb2[:, t0:t1, :], ALU.subtract)
+
+        def gates(t0, t1):
+            nc.scalar.activation(sp[:, t0:t1, :], diff[:, t0:t1, :], ACT.Sigmoid)
+            nc.scalar.activation(sn[:, t0:t1, :], diff[:, t0:t1, :], ACT.Sigmoid, scale=-1.0)
+
+        for h in range(2):
+            nc.scalar.copy(y[0][:, cols(h)], first[h][:])
+        nc.vector.tensor_copy(pa[:, 0, :], y[0][:].indirect(l1[:]))
+        gather_s(pb[:, 0, :], y[0], l2[:])
+        order_pairs(0, 1)
+        nc.vector.tensor_copy(w2w[:], dealt(w2w_raw[:]))
+        nc.vector.tensor_copy(w2s[:], dealt(w2s_raw[:]))
+        nc.scalar.copy(y[1][:], yacc[1][:])
+        fetch_a(1)
+        order_pairs(1, 2)
+        nc.scalar.copy(y[2][:], yacc[2][:])
+        fetch_b(0)
+        fetch_b(1)
+        difference(0, 2)
+        nc.scalar.copy(y[3][:], yacc[3][:])
+        fetch_a(2)
+        fetch_a(3)
+        order_pairs(2, 4)
+        fetch_b(2)
+        fetch_b(3)
+        difference(2, 4)
+
+        zc = [sb("zc%d" % h, [P, PACK, HALF], BF16, tag="hold%d" % (1 + h)) for h in range(2)]
+        zi = [sb("zi%d" % h, [P, HALF, PACK], BF16, tag="hold%d" % (3 + h)) for h in range(2)]
+
+        def round_z(t):
+            for h in range(2):
+                nc.scalar.activation(zc[h][:, t, :], dt[t][:, cols(h)], ACT.Copy, scale=gain[:, t:t + 1])
+
+        round_z(0)
+        round_z(1)
+        gates(0, 2)
+        round_z(2)
+        round_z(3)
+
+        def scatter_b(window, t, which):
+            if which == 0:
+                nc.vector.tensor_tensor(window[:].indirect(l3[:]), pa2[:, t, :], sp[:, t, :], ALU.mult)
+            else:
+                nc.vector.tensor_tensor(window[:].indirect(l4[:]), pb2[:, t, :], sn[:, t, :], ALU.mult)
+
+        dt2 = [sb("dt2_0", [P, S], F32)]
+        scatter_b(dt2[0], 0, 0)
+        scatter_b(dt2[0], 0, 1)
+
+        zw = sb("zw", [P, S], U32)
+        zs = sb("zs", [P, S], U8)
+        for h in range(2):
+            weave(nc.scalar.copy, zi[h][:], zc[h][:])
+            nc.vector.quantize_mx(out=zw[:, cols(h)].bitcast(FP8X4), scales=zs[:, cols(h)],
+                                  in_=zi[h][:].rearrange("p c t -> p (c t)"))
+        gates(2, 4)
+        for t in range(1, PACK):
+            dt2.append(sb("dt2_%d" % t, [P, S], F32, tag="hold%d" % (2, 4, 3)[t - 1]))
+        for t, which in ((1, 0), (2, 0), (1, 1), (3, 0), (2, 1), (3, 1)):
+            scatter_b(dt2[t], t, which)
+
+        a = [sb("a%d" % t, [P, S], F32) for t in range(PACK)]
+        for t in range(PACK):
+            nc.scalar.copy(a[t][:], product("aacc%d" % t, w2w, w2s, t, zw[:], zs[:])[:])
+
+        z2c = sb("z2c", [P, PACK, S], BF16)
+        a5 = [sb("a5_%d" % h, [P, PACK, HALF], F32) for h in range(2)]
+        a6 = [sb("a6_%d" % h, [P, PACK, HALF], F32) for h in range(2)]
+
+        def round_z2(t):
+            nc.scalar.activation(z2c[:, t, :], dt2[t][:], ACT.Copy, scale=gain[:, t:t + 1])
+
+        def fetch_half(dst, windows, lst, h, ts):
+            for t in ts:
+                gather_s(dst[h][:, t, :], windows[t], half_of(lst, h))
+
+        round_z2(0)
+        fetch_half(a5, a, l5, 0, range(PACK))
+        round_z2(1)
+        fetch_half(a5, a, l5, 1, range(PACK))
+        round_z2(2)
+        fetch_half(a6, a, l6, 0, range(PACK))
+
+        nc.vector.tensor_scalar(z2c[:, 3, :], dt2[3][:], gain[:, 3:4], None, ALU.mult)
+        z2i = [sb("z2i%d" % h, [P, HALF, PACK], BF16) for h in range(2)]
+        z2w = sb("z2w", [P, S], U32)
+        z2s = sb("z2s", [P, S], U8)
+        for h in range(2):
+            weave(nc.vector.tensor_copy, z2i[h][:], z2c[:, :, cols(h)])
+        for h in range(2):
+            nc.vector.quantize_mx(out=z2w[:, cols(h)].bitcast(FP8X4), scales=z2s[:, cols(h)],
+                                  in_=z2i[h][:].rearrange("p c t -> p (c t)"))
+        b = [sb("b%d" % t, [P, S], F32) for t in range(PACK)]
+        for h in range(2):
+            for t in range(PACK):
+                nc.scalar.copy(b[t][:, cols(h)], product("bacc%d_%d" % (t, h), w2w, w2s, t, z2w[:, cols(h)], z2s[:, cols(h)])[:])
+
+        s1 = [sb("s1_%d" % h, [P, PACK, HALF], F32) for h in range(2)]
+        s2 = [sb("s2_%d" % h, [P, PACK, HALF], F32) for h in range(2)]
+        b8 = [sb("b8_%d" % h, [P, PACK, HALF], F32) for h in range(2)]
+        res = [sb("res%d" % h, [P, PACK, HALF], F32) for h in range(2)]
+        oi = [sb("oi%d" % h, [P, HALF, PACK], BF16) for h in range(2)]
+        ow = sb("ow", [P, S], U32)
+        osc = sb("osc", [P, S], U8)
+        fused = (0, 0)
+
+        fetch_half(b8, b, l8, 0, range(fused[0], PACK))
+        fetch_half(a6, a, l6, 1, range(PACK))
+        fetch_half(b8, b, l8, 1, range(fused[1], PACK))
+        for h in range(2):
+            for t in range(PACK):
+                nc.vector.tensor_tensor(s1[h][:, t, :], b[t][:].indirect(half_of(l7, h)), a5[h][:, t, :], ALU.add)
+        out0_rows = out_0.rearrange("(p t) c -> p t c", t=PACK)
+        out1_words = words_of(out_1)
+        for h in range(2):
+            for t in range(fused[h]):
+                nc.vector.tensor_tensor(s2[h][:, t, :], b[t][:].indirect(half_of(l8, h)), a6[h][:, t, :], ALU.add)
+            nc.vector.tensor_tensor(s2[h][:, fused[h]:, :], b8[h][:, fused[h]:, :], a6[h][:, fused[h]:, :], ALU.add)
+            nc.vector.tensor_tensor(res[h][:], s1[h][:], s2[h][:], ALU.max)
+            nc.sync.dma_start(out0_rows[:, :, cols(h)], res[h][:])
+            weave(nc.scalar.copy if h == 0 else nc.vector.tensor_copy, oi[h][:], res[h][:])
+        for h in range(2):
+            nc.vector.quantize_mx(out=ow[:, cols(h)].bitcast(FP8X4), scales=osc[:, cols(h)],
+                                  in_=oi[h][:].rearrange("p c t -> p (c t)"))
+            nc.sync.dma_start(out1_words[:, cols(h)], ow[:, cols(h)].bitcast(I32))
+        for q in range(4):
+            queue = nc.sync if q % 2 else nc.scalar
+            queue.dma_start(out_2[0, 4 * q:4 * q + 4, :].bitcast(I32), osc[32 * q:32 * q + 4, :].bitcast(I32))

@@ -18,6 +18,8 @@ T = 2048
 S = 512
 W = 256
 HALF = S // 2
+PIECES = ((0, 384), (384, 512))
+FUSED = (4, 4)
 FLOPS = 3 * 2 * 512 * 512 * 512
 
 
@@ -29,6 +31,7 @@ def tile_picked_tiepathborderduel_none_po_kernel(
     with ExitStack() as ctx:
         lists = ctx.enter_context(tc.tile_pool(name="lists", bufs=1))
         keep = ctx.enter_context(tc.tile_pool(name="keep", bufs=1))
+        reuse = ctx.enter_context(tc.tile_pool(name="reuse", bufs=1))
         psum = ctx.enter_context(tc.psum_pool(name="psum", bufs=8))
 
         def sb(name, shape, dtype, tag=None):
@@ -69,8 +72,8 @@ def tile_picked_tiepathborderduel_none_po_kernel(
         xs = sb("xs", [P, T], U8)
         w1s_raw = sb("w1s_raw", [P, S], U8)
         w2s_raw = sb("w2s_raw", [P, S], U8)
-        nc.gpsimd.memset(xs[:].bitcast(I32), 0)
-        nc.vector.memset(w1s_raw[:].bitcast(I32), 0)
+        nc.vector.memset(xs[:].bitcast(I32), 0)
+        nc.gpsimd.memset(w1s_raw[:].bitcast(I32), 0)
         nc.vector.memset(w2s_raw[:].bitcast(I32), 0)
         l_offs = load_list("l_offs", offs)
         l1 = load_list("l1", n1)
@@ -102,10 +105,11 @@ def tile_picked_tiepathborderduel_none_po_kernel(
         w1w = sb("w1w", [P, PACK, P], I32)
         nc.vector.tensor_copy(xgs[:], xs[:].indirect(l_offs[:]))
         nc.vector.tensor_copy(xg[:, cols(0)], xw[:].indirect(half_of(l_offs, 0)))
-        nc.vector.tensor_copy(w1w[:, 0, :], dealt(w1w_raw[:])[:, 0, :])
-        nc.vector.tensor_copy(w1s[:], dealt(w1s_raw[:]))
+        nc.gpsimd.tensor_copy(w1w[:, 0, :], dealt(w1w_raw[:])[:, 0, :])
+        nc.gpsimd.tensor_copy(w1s[:, 0, :], dealt(w1s_raw[:])[:, 0, :])
         nc.vector.tensor_copy(xg[:, cols(1)], xw[:].indirect(half_of(l_offs, 1)))
         nc.vector.tensor_copy(w1w[:, 1:, :], dealt(w1w_raw[:])[:, 1:, :])
+        nc.vector.tensor_copy(w1s[:, 1:, :], dealt(w1s_raw[:])[:, 1:, :])
 
         y = [sb("y%d" % t, [P, S], F32) for t in range(PACK)]
         first = [product("y0_%d" % h, w1w, w1s, 0, xg[:, cols(h)], xgs[:, cols(h)]) for h in range(2)]
@@ -120,7 +124,7 @@ def tile_picked_tiepathborderduel_none_po_kernel(
         rb = sb("rb", [P, PACK, W], F32)
         pa2 = sb("pa2", [P, PACK, W], F32)
         pb2 = sb("pb2", [P, PACK, W], F32)
-        diff = sb("diff", [P, PACK, W], F32)
+        diff = [reuse.tile([P, 2, W], F32, name="diff0", align_bytes=64, offset=0), sb("diff1", [P, 2, W], F32)]
         sp = sb("sp", [P, PACK, W], F32)
         sn = sb("sn", [P, PACK, W], F32)
         dt = [sb("dt%d" % t, [P, S], F32) for t in range(PACK)]
@@ -142,44 +146,47 @@ def tile_picked_tiepathborderduel_none_po_kernel(
             gather_s(pb2[:, t, :], y[t], l4[:])
 
         def difference(t0, t1):
-            nc.vector.tensor_tensor(diff[:, t0:t1, :], pa2[:, t0:t1, :], pb2[:, t0:t1, :], ALU.subtract)
+            nc.gpsimd.tensor_tensor(diff[t0 // 2][:, t0 % 2:t0 % 2 + t1 - t0, :], pa2[:, t0:t1, :], pb2[:, t0:t1, :], ALU.subtract)
 
         def gates(t0, t1):
-            nc.scalar.activation(sp[:, t0:t1, :], diff[:, t0:t1, :], ACT.Sigmoid)
-            nc.scalar.activation(sn[:, t0:t1, :], diff[:, t0:t1, :], ACT.Sigmoid, scale=-1.0)
+            nc.scalar.activation(sp[:, t0:t1, :], diff[t0 // 2][:], ACT.Sigmoid)
+            nc.scalar.activation(sn[:, t0:t1, :], diff[t0 // 2][:], ACT.Sigmoid, scale=-1.0)
 
         for h in range(2):
             nc.scalar.copy(y[0][:, cols(h)], first[h][:])
         nc.vector.tensor_copy(pa[:, 0, :], y[0][:].indirect(l1[:]))
         gather_s(pb[:, 0, :], y[0], l2[:])
         order_pairs(0, 1)
-        nc.vector.tensor_copy(w2w[:], dealt(w2w_raw[:]))
-        nc.vector.tensor_copy(w2s[:], dealt(w2s_raw[:]))
         nc.scalar.copy(y[1][:], yacc[1][:])
         fetch_a(1)
         order_pairs(1, 2)
         nc.scalar.copy(y[2][:], yacc[2][:])
         fetch_b(0)
         fetch_b(1)
-        difference(0, 2)
+        difference(0, 1)
+        difference(1, 2)
         nc.scalar.copy(y[3][:], yacc[3][:])
         fetch_a(2)
         fetch_a(3)
         order_pairs(2, 4)
         fetch_b(2)
         fetch_b(3)
-        difference(2, 4)
+        difference(2, 3)
+        difference(3, 4)
+        for t in range(PACK):
+            nc.gpsimd.tensor_copy(w2w[:, t, :], dealt(w2w_raw[:])[:, t, :])
+            nc.gpsimd.tensor_copy(w2s[:, t, :], dealt(w2s_raw[:])[:, t, :])
 
-        zc = [sb("zc%d" % h, [P, PACK, HALF], BF16, tag="hold%d" % (1 + h)) for h in range(2)]
-        zi = [sb("zi%d" % h, [P, HALF, PACK], BF16, tag="hold%d" % (3 + h)) for h in range(2)]
+        gates(0, 2)
+        zc = reuse.tile([P, PACK, S], BF16, name="zc", align_bytes=64, offset=0)
+        zi = reuse.tile([P, S, PACK], BF16, name="zi", align_bytes=64, offset=4096)
 
         def round_z(t):
-            for h in range(2):
-                nc.scalar.activation(zc[h][:, t, :], dt[t][:, cols(h)], ACT.Copy, scale=gain[:, t:t + 1])
+            nc.scalar.activation(zc[:, t, :], dt[t][:], ACT.Copy, scale=gain[:, t:t + 1])
 
         round_z(0)
         round_z(1)
-        gates(0, 2)
+        gates(2, 4)
         round_z(2)
         round_z(3)
 
@@ -195,37 +202,42 @@ def tile_picked_tiepathborderduel_none_po_kernel(
 
         zw = sb("zw", [P, S], U32)
         zs = sb("zs", [P, S], U8)
-        for h in range(2):
-            weave(nc.scalar.copy, zi[h][:], zc[h][:])
-            nc.vector.quantize_mx(out=zw[:, cols(h)].bitcast(FP8X4), scales=zs[:, cols(h)],
-                                  in_=zi[h][:].rearrange("p c t -> p (c t)"))
-        gates(2, 4)
+        weave(nc.scalar.copy, zi[:], zc[:])
+        nc.vector.quantize_mx(out=zw[:].bitcast(FP8X4), scales=zs[:], in_=zi[:].rearrange("p c t -> p (c t)"))
         for t in range(1, PACK):
-            dt2.append(sb("dt2_%d" % t, [P, S], F32, tag="hold%d" % (2, 4, 3)[t - 1]))
+            dt2.append(reuse.tile([P, S], F32, name="dt2_%d" % t, align_bytes=64, offset=2048 * (t - 1)))
         for t, which in ((1, 0), (2, 0), (1, 1), (3, 0), (2, 1), (3, 1)):
             scatter_b(dt2[t], t, which)
 
-        a = [sb("a%d" % t, [P, S], F32) for t in range(PACK)]
-        for t in range(PACK):
-            nc.scalar.copy(a[t][:], product("aacc%d" % t, w2w, w2s, t, zw[:], zs[:])[:])
+        z2c = reuse.tile([P, PACK, S], BF16, name="z2c", align_bytes=64, offset=6144)
+        npieces = len(PIECES)
 
-        z2c = sb("z2c", [P, PACK, S], BF16)
-        a5 = [sb("a5_%d" % h, [P, PACK, HALF], F32) for h in range(2)]
-        a6 = [sb("a6_%d" % h, [P, PACK, HALF], F32) for h in range(2)]
+        def piece_tiles(name, dtype=F32):
+            return [sb("%s_%d" % (name, k), [P, PACK, hi - lo], dtype) for k, (lo, hi) in enumerate(PIECES)]
+
+        def piece_of(lst, k):
+            lo, hi = PIECES[k]
+            return lst[:, lo // 16:hi // 16]
+
+        a5, a6 = piece_tiles("a5"), piece_tiles("a6")
 
         def round_z2(t):
             nc.scalar.activation(z2c[:, t, :], dt2[t][:], ACT.Copy, scale=gain[:, t:t + 1])
 
-        def fetch_half(dst, windows, lst, h, ts):
+        def fetch_piece(dst, windows, lst, k, ts):
             for t in ts:
-                gather_s(dst[h][:, t, :], windows[t], half_of(lst, h))
+                gather_s(dst[k][:, t, :], windows[t], piece_of(lst, k))
 
         round_z2(0)
-        fetch_half(a5, a, l5, 0, range(PACK))
+        a = [sb("a%d" % t, [P, S], F32) for t in range(PACK)]
+        for t in range(PACK):
+            nc.scalar.copy(a[t][:], product("aacc%d" % t, w2w, w2s, t, zw[:], zs[:])[:])
+
+        fetch_piece(a5, a, l5, 0, range(PACK))
         round_z2(1)
-        fetch_half(a5, a, l5, 1, range(PACK))
+        fetch_piece(a6, a, l6, 0, range(2))
         round_z2(2)
-        fetch_half(a6, a, l6, 0, range(PACK))
+        fetch_piece(a6, a, l6, 0, range(2, PACK))
 
         nc.vector.tensor_scalar(z2c[:, 3, :], dt2[3][:], gain[:, 3:4], None, ALU.mult)
         z2i = [sb("z2i%d" % h, [P, HALF, PACK], BF16) for h in range(2)]
@@ -239,36 +251,36 @@ def tile_picked_tiepathborderduel_none_po_kernel(
         b = [sb("b%d" % t, [P, S], F32) for t in range(PACK)]
         for h in range(2):
             for t in range(PACK):
-                nc.scalar.copy(b[t][:, cols(h)], product("bacc%d_%d" % (t, h), w2w, w2s, t, z2w[:, cols(h)], z2s[:, cols(h)])[:])
+                copy_out = nc.vector.tensor_copy if (h, t) in ((0, 2), (0, 3), (1, 0)) else nc.scalar.copy
+                copy_out(b[t][:, cols(h)], product("bacc%d_%d" % (t, h), w2w, w2s, t, z2w[:, cols(h)], z2s[:, cols(h)])[:])
 
-        s1 = [sb("s1_%d" % h, [P, PACK, HALF], F32) for h in range(2)]
-        s2 = [sb("s2_%d" % h, [P, PACK, HALF], F32) for h in range(2)]
-        b8 = [sb("b8_%d" % h, [P, PACK, HALF], F32) for h in range(2)]
-        res = [sb("res%d" % h, [P, PACK, HALF], F32) for h in range(2)]
-        oi = [sb("oi%d" % h, [P, HALF, PACK], BF16) for h in range(2)]
+        s1, s2, b7, b8, res = (piece_tiles(name) for name in ("s1", "s2", "b7", "b8", "res"))
+        oi = [sb("oi%d" % k, [P, hi - lo, PACK], BF16) for k, (lo, hi) in enumerate(PIECES)]
         ow = sb("ow", [P, S], U32)
         osc = sb("osc", [P, S], U8)
-        fused = (0, 0)
-
-        fetch_half(b8, b, l8, 0, range(fused[0], PACK))
-        fetch_half(a6, a, l6, 1, range(PACK))
-        fetch_half(b8, b, l8, 1, range(fused[1], PACK))
-        for h in range(2):
-            for t in range(PACK):
-                nc.vector.tensor_tensor(s1[h][:, t, :], b[t][:].indirect(half_of(l7, h)), a5[h][:, t, :], ALU.add)
         out0_rows = out_0.rearrange("(p t) c -> p t c", t=PACK)
         out1_words = words_of(out_1)
-        for h in range(2):
-            for t in range(fused[h]):
-                nc.vector.tensor_tensor(s2[h][:, t, :], b[t][:].indirect(half_of(l8, h)), a6[h][:, t, :], ALU.add)
-            nc.vector.tensor_tensor(s2[h][:, fused[h]:, :], b8[h][:, fused[h]:, :], a6[h][:, fused[h]:, :], ALU.add)
-            nc.vector.tensor_tensor(res[h][:], s1[h][:], s2[h][:], ALU.max)
-            nc.sync.dma_start(out0_rows[:, :, cols(h)], res[h][:])
-            weave(nc.scalar.copy if h == 0 else nc.vector.tensor_copy, oi[h][:], res[h][:])
-        for h in range(2):
-            nc.vector.quantize_mx(out=ow[:, cols(h)].bitcast(FP8X4), scales=osc[:, cols(h)],
-                                  in_=oi[h][:].rearrange("p c t -> p (c t)"))
-            nc.sync.dma_start(out1_words[:, cols(h)], ow[:, cols(h)].bitcast(I32))
+
+        for k in range(npieces):
+            if k > 0:
+                fetch_piece(a5, a, l5, k, range(PACK))
+                fetch_piece(a6, a, l6, k, range(PACK))
+            fetch_piece(b8, b, l8, k, range(PACK))
+            fetch_piece(b7, b, l7, k, range(FUSED[k], PACK))
+        for k, (lo, hi) in enumerate(PIECES):
+            f = FUSED[k]
+            for t in range(f):
+                nc.vector.tensor_tensor(s1[k][:, t, :], b[t][:].indirect(piece_of(l7, k)), a5[k][:, t, :], ALU.add)
+            nc.vector.tensor_tensor(s2[k][:], b8[k][:], a6[k][:], ALU.add)
+            if f < PACK:
+                nc.vector.tensor_tensor(s1[k][:, f:, :], b7[k][:, f:, :], a5[k][:, f:, :], ALU.add)
+            nc.vector.tensor_tensor(res[k][:], s1[k][:], s2[k][:], ALU.max)
+            nc.sync.dma_start(out0_rows[:, :, lo:hi], res[k][:])
+            weave(nc.scalar.copy if k < npieces - 1 else nc.vector.tensor_copy, oi[k][:], res[k][:])
+        for k, (lo, hi) in enumerate(PIECES):
+            nc.vector.quantize_mx(out=ow[:, lo:hi].bitcast(FP8X4), scales=osc[:, lo:hi],
+                                  in_=oi[k][:].rearrange("p c t -> p (c t)"))
+            nc.sync.dma_start(out1_words[:, lo:hi], ow[:, lo:hi].bitcast(I32))
         for q in range(4):
             queue = nc.sync if q % 2 else nc.scalar
             queue.dma_start(out_2[0, 4 * q:4 * q + 4, :].bitcast(I32), osc[32 * q:32 * q + 4, :].bitcast(I32))

@@ -14,12 +14,23 @@ ACT = mybir.ActivationFunctionType
 
 P = 128
 PACK = 4
+QUADRANTS = 4
 T = 2048
 S = 512
 W = 256
 HALF = S // 2
+PER_COLUMN = 16
+
 PIECES = ((0, 384), (384, 512))
-FUSED = (4, 4)
+OUT_RANGES = ((0, 0, 256), (1, 384, 512), (0, 256, 384))
+
+AT_RA = 0
+AT_DT3 = 5120
+AT_ZI = 8192
+AT_RB2_0 = AT_ZI - 512
+AT_DT2_2 = AT_ZI + 512
+AT_DT2_3 = AT_DT2_2 + 2048
+
 FLOPS = 3 * 2 * 512 * 512 * 512
 
 
@@ -34,40 +45,53 @@ def tile_picked_tiepathborderduel_none_po_kernel(
         reuse = ctx.enter_context(tc.tile_pool(name="reuse", bufs=1))
         psum = ctx.enter_context(tc.psum_pool(name="psum", bufs=8))
 
-        def sb(name, shape, dtype, tag=None):
-            return keep.tile(shape, dtype, name=name, tag=tag or name, align_bytes=64)
+        def sb(name, shape, dtype):
+            return keep.tile(shape, dtype, name=name, tag=name, align_bytes=64)
+
+        def placed(name, shape, dtype, offset):
+            return reuse.tile(shape, dtype, name=name, align_bytes=64, offset=offset)
 
         def load_list(name, src):
             tile = lists.tile(list(src.shape), U16, name=name)
             nc.sync.dma_start(tile[:], src)
             return tile
 
-        def half_of(lst, h):
-            return lst[:, h * (HALF // 16):(h + 1) * (HALF // 16)]
+        def entries(lst, lo, hi):
+            return lst[:, lo // PER_COLUMN:hi // PER_COLUMN]
 
         def cols(h):
             return slice(h * HALF, (h + 1) * HALF)
 
-        def words_of(src):
-            return src[0].rearrange("p n t -> p (n t)").bitcast(I32)
+        def words_of(dram):
+            return dram[0].rearrange("p n t -> p (n t)").bitcast(I32)
 
-        def load_scale_rows(queue, plane, src, q):
-            queue.dma_start(plane[32 * q:32 * q + 4, :].bitcast(I32), src[0, 4 * q:4 * q + 4, :].bitcast(I32))
+        def scale_rows(dram, q):
+            return dram[0, 4 * q:4 * q + 4, :].bitcast(I32)
+
+        def live_rows(scales, q):
+            return scales[32 * q:32 * q + 4, :].bitcast(I32)
 
         def dealt(ap):
             return ap.rearrange("p (m t) -> p t m", t=PACK)
 
-        def product(name, ww, ws, t, words, plane):
+        def product(name, ww, ws, t, words, scales):
             acc = psum.tile([P, words.shape[1]], F32, name=name, tag="acc")
             nc.tensor.matmul_mx(out=acc[:], lhsT=ww[:, t, :].bitcast(FP8X4), lhsT_scale=ws[:, t, :],
-                                rhs=words.bitcast(FP8X4), rhs_scale=plane, start=True, stop=True)
+                                rhs=words.bitcast(FP8X4), rhs_scale=scales, start=True, stop=True)
             return acc
 
-        def gather_s(out, window, lst):
-            nc.scalar.activation(out, window[:].indirect(lst), ACT.Copy)
+        def scalar_gather(out, window, offsets):
+            nc.scalar.activation(out, window[:].indirect(offsets), ACT.Copy)
 
-        def weave(engine_copy, dst, src):
+        def scatter(window, lst, values):
+            nc.vector.tensor_copy(window[:].indirect(lst[:]), values)
+
+        def interleave(engine_copy, dst, src):
             engine_copy(dst.rearrange("p (c i) t -> p c t i", i=4), src.rearrange("p t (c i) -> p c t i", i=4))
+
+        def quantise(words, scales, interleaved):
+            nc.vector.quantize_mx(out=words.bitcast(FP8X4), scales=scales,
+                                  in_=interleaved.rearrange("p c t -> p (c t)"))
 
         xs = sb("xs", [P, T], U8)
         w1s_raw = sb("w1s_raw", [P, S], U8)
@@ -80,20 +104,21 @@ def tile_picked_tiepathborderduel_none_po_kernel(
         l2 = load_list("l2", n2)
         xw = sb("xw", [P, T], U32)
         nc.sync.dma_start(xw[:].bitcast(I32), words_of(x_words))
-        for q in range(4):
-            load_scale_rows(nc.scalar, xs, x_scales, q)
+        for q in range(QUADRANTS):
+            nc.scalar.dma_start(live_rows(xs, q), scale_rows(x_scales, q))
         w1w_raw = sb("w1w_raw", [P, S], I32)
         nc.sync.dma_start(w1w_raw[:], words_of(w1_words))
-        for q in range(4):
-            load_scale_rows(nc.scalar if q < 2 else nc.gpsimd, w1s_raw, w1_scales, q)
+        for q in range(QUADRANTS):
+            queue = nc.scalar if q < QUADRANTS // 2 else nc.gpsimd
+            queue.dma_start(live_rows(w1s_raw, q), scale_rows(w1_scales, q))
         w2w_raw = sb("w2w_raw", [P, S], I32)
         nc.sync.dma_start(w2w_raw[:], words_of(w2_words))
         l3 = load_list("l3", n3)
         l4 = load_list("l4", n4)
         gain = sb("gain", [P, PACK], F32)
         nc.sync.dma_start(gain[:], gn.rearrange("(p t) o -> p (t o)", t=PACK))
-        for q in range(4):
-            load_scale_rows(nc.sync, w2s_raw, w2_scales, q)
+        for q in range(QUADRANTS):
+            nc.sync.dma_start(live_rows(w2s_raw, q), scale_rows(w2_scales, q))
         l5 = load_list("l5", n5)
         l6 = load_list("l6", n6)
         l7 = load_list("l7", n7)
@@ -104,183 +129,207 @@ def tile_picked_tiepathborderduel_none_po_kernel(
         w1s = sb("w1s", [P, PACK, P], U8)
         w1w = sb("w1w", [P, PACK, P], I32)
         nc.vector.tensor_copy(xgs[:], xs[:].indirect(l_offs[:]))
-        nc.vector.tensor_copy(xg[:, cols(0)], xw[:].indirect(half_of(l_offs, 0)))
+        nc.vector.tensor_copy(xg[:, cols(0)], xw[:].indirect(entries(l_offs, 0, HALF)))
         nc.gpsimd.tensor_copy(w1w[:, 0, :], dealt(w1w_raw[:])[:, 0, :])
         nc.gpsimd.tensor_copy(w1s[:, 0, :], dealt(w1s_raw[:])[:, 0, :])
-        nc.vector.tensor_copy(xg[:, cols(1)], xw[:].indirect(half_of(l_offs, 1)))
+        nc.vector.tensor_copy(xg[:, cols(1)], xw[:].indirect(entries(l_offs, HALF, S)))
         nc.vector.tensor_copy(w1w[:, 1:, :], dealt(w1w_raw[:])[:, 1:, :])
         nc.vector.tensor_copy(w1s[:, 1:, :], dealt(w1s_raw[:])[:, 1:, :])
 
         y = [sb("y%d" % t, [P, S], F32) for t in range(PACK)]
-        first = [product("y0_%d" % h, w1w, w1s, 0, xg[:, cols(h)], xgs[:, cols(h)]) for h in range(2)]
-        yacc = [None] + [product("yacc%d" % t, w1w, w1s, t, xg[:], xgs[:]) for t in range(1, PACK)]
+        y0_acc = [product("y0_%d" % h, w1w, w1s, 0, xg[:, cols(h)], xgs[:, cols(h)]) for h in range(2)]
+        y_acc = {t: product("yacc%d" % t, w1w, w1s, t, xg[:], xgs[:]) for t in range(1, PACK)}
 
         w2s = sb("w2s", [P, PACK, P], U8)
         w2w = sb("w2w", [P, PACK, P], I32)
 
         pa = sb("pa", [P, PACK, W], F32)
         pb = sb("pb", [P, PACK, W], F32)
-        ra = sb("ra", [P, PACK, W], F32)
+        ra = placed("ra", [P, PACK, W], F32, AT_RA)
         rb = sb("rb", [P, PACK, W], F32)
         pa2 = sb("pa2", [P, PACK, W], F32)
         pb2 = sb("pb2", [P, PACK, W], F32)
-        diff = [reuse.tile([P, 2, W], F32, name="diff0", align_bytes=64, offset=0), sb("diff1", [P, 2, W], F32)]
+        diff0 = placed("diff0", [P, 1, W], F32, AT_ZI)
+        diff123 = sb("diff123", [P, PACK - 1, W], F32)
+        ra2 = sb("ra2", [P, PACK, W], F32)
+        rb2 = {t: sb("rb2_%d" % t, [P, W], F32) for t in range(1, PACK)}
         sp = sb("sp", [P, PACK, W], F32)
         sn = sb("sn", [P, PACK, W], F32)
-        dt = [sb("dt%d" % t, [P, S], F32) for t in range(PACK)]
+        dt = [sb("dt%d" % t, [P, S], F32) for t in range(PACK - 1)] + [placed("dt3", [P, S], F32, AT_DT3)]
 
-        def order_pairs(t0, t1):
+        def larger(t0, t1):
             nc.vector.tensor_tensor(ra[:, t0:t1, :], pa[:, t0:t1, :], pb[:, t0:t1, :], ALU.max)
+
+        def smaller(t0, t1):
             nc.vector.tensor_tensor(rb[:, t0:t1, :], pa[:, t0:t1, :], pb[:, t0:t1, :], ALU.min)
-            for t in range(t0, t1):
-                nc.vector.tensor_copy(dt[t][:].indirect(l1[:]), ra[:, t, :])
-            for t in range(t0, t1):
-                nc.vector.tensor_copy(dt[t][:].indirect(l2[:]), rb[:, t, :])
 
-        def fetch_a(t):
-            gather_s(pa[:, t, :], y[t], l1[:])
-            gather_s(pb[:, t, :], y[t], l2[:])
+        def put_ra(t):
+            scatter(dt[t], l1, ra[:, t, :])
 
-        def fetch_b(t):
-            gather_s(pa2[:, t, :], y[t], l3[:])
-            gather_s(pb2[:, t, :], y[t], l4[:])
+        def put_rb(t):
+            scatter(dt[t], l2, rb[:, t, :])
 
-        def difference(t0, t1):
-            nc.gpsimd.tensor_tensor(diff[t0 // 2][:, t0 % 2:t0 % 2 + t1 - t0, :], pa2[:, t0:t1, :], pb2[:, t0:t1, :], ALU.subtract)
+        def fetch_pa_pb(t):
+            scalar_gather(pa[:, t, :], y[t], l1[:])
+            scalar_gather(pb[:, t, :], y[t], l2[:])
 
-        def gates(t0, t1):
-            nc.scalar.activation(sp[:, t0:t1, :], diff[t0 // 2][:], ACT.Sigmoid)
-            nc.scalar.activation(sn[:, t0:t1, :], diff[t0 // 2][:], ACT.Sigmoid, scale=-1.0)
+        def fetch_pa2_pb2(t):
+            scalar_gather(pa2[:, t, :], y[t], l3[:])
+            scalar_gather(pb2[:, t, :], y[t], l4[:])
+
+        def diff(t0, t1):
+            return diff0[:] if t0 == 0 else diff123[:, t0 - 1:t1 - 1, :]
+
+        def subtract(t):
+            nc.gpsimd.tensor_tensor(diff(t, t + 1), pa2[:, t:t + 1, :], pb2[:, t:t + 1, :], ALU.subtract)
+
+        def sigmoids(t0, t1):
+            nc.scalar.activation(sp[:, t0:t1, :], diff(t0, t1), ACT.Sigmoid)
+            nc.scalar.activation(sn[:, t0:t1, :], diff(t0, t1), ACT.Sigmoid, scale=-1.0)
+
+        def make_ra2(t):
+            nc.gpsimd.tensor_tensor(ra2[:, t, :], pa2[:, t, :], sp[:, t, :], ALU.mult)
+
+        def make_rb2(t):
+            nc.gpsimd.tensor_tensor(rb2[t][:], pb2[:, t, :], sn[:, t, :], ALU.mult)
+
+        def gpsimd_round(out, window, t):
+            nc.gpsimd.tensor_scalar(out, window[:], gain[:, t:t + 1], 0.0, ALU.mult, ALU.add)
 
         for h in range(2):
-            nc.scalar.copy(y[0][:, cols(h)], first[h][:])
+            nc.scalar.copy(y[0][:, cols(h)], y0_acc[h][:])
         nc.vector.tensor_copy(pa[:, 0, :], y[0][:].indirect(l1[:]))
-        gather_s(pb[:, 0, :], y[0], l2[:])
-        order_pairs(0, 1)
-        nc.scalar.copy(y[1][:], yacc[1][:])
-        fetch_a(1)
-        order_pairs(1, 2)
-        nc.scalar.copy(y[2][:], yacc[2][:])
-        fetch_b(0)
-        fetch_b(1)
-        difference(0, 1)
-        difference(1, 2)
-        nc.scalar.copy(y[3][:], yacc[3][:])
-        fetch_a(2)
-        fetch_a(3)
-        order_pairs(2, 4)
-        fetch_b(2)
-        fetch_b(3)
-        difference(2, 3)
-        difference(3, 4)
+        scalar_gather(pb[:, 0, :], y[0], l2[:])
+        larger(0, 1)
+        put_ra(0)
+        nc.scalar.copy(y[1][:], y_acc[1][:])
+        fetch_pa_pb(1)
+        larger(1, 2)
+        smaller(0, 2)
+        put_ra(1)
+        put_rb(0)
+        put_rb(1)
+        nc.scalar.copy(y[2][:], y_acc[2][:])
+        fetch_pa2_pb2(0)
+        subtract(0)
+        nc.scalar.copy(y[3][:], y_acc[3][:])
+        fetch_pa_pb(2)
+        fetch_pa_pb(3)
+        larger(2, 4)
+        smaller(2, 4)
+        for put in (put_ra, put_rb):
+            put(2)
+            put(3)
+
+        fetch_pa2_pb2(1)
+        subtract(1)
+        sigmoids(0, 1)
+        sigmoids(1, 2)
+        make_ra2(0)
+        zi = placed("zi", [P, S, PACK], BF16, AT_ZI)
+        for t in range(2):
+            gpsimd_round(zi[:, :, t], dt[t], t)
+        make_ra2(1)
+        make_rb2(1)
+        for t in range(2, PACK):
+            fetch_pa2_pb2(t)
+            subtract(t)
         for t in range(PACK):
             nc.gpsimd.tensor_copy(w2w[:, t, :], dealt(w2w_raw[:])[:, t, :])
             nc.gpsimd.tensor_copy(w2s[:, t, :], dealt(w2s_raw[:])[:, t, :])
+        for t in range(2, PACK):
+            nc.scalar.activation(zi[:, :, t], dt[t][:], ACT.Copy, scale=gain[:, t:t + 1])
+        sigmoids(2, 4)
 
-        gates(0, 2)
-        zc = reuse.tile([P, PACK, S], BF16, name="zc", align_bytes=64, offset=0)
-        zi = reuse.tile([P, S, PACK], BF16, name="zi", align_bytes=64, offset=4096)
-
-        def round_z(t):
-            nc.scalar.activation(zc[:, t, :], dt[t][:], ACT.Copy, scale=gain[:, t:t + 1])
-
-        round_z(0)
-        round_z(1)
-        gates(2, 4)
-        round_z(2)
-        round_z(3)
-
-        def scatter_b(window, t, which):
-            if which == 0:
-                nc.vector.tensor_tensor(window[:].indirect(l3[:]), pa2[:, t, :], sp[:, t, :], ALU.mult)
-            else:
-                nc.vector.tensor_tensor(window[:].indirect(l4[:]), pb2[:, t, :], sn[:, t, :], ALU.mult)
-
-        dt2 = [sb("dt2_0", [P, S], F32)]
-        scatter_b(dt2[0], 0, 0)
-        scatter_b(dt2[0], 0, 1)
-
+        dt2 = [placed("dt2_0", [P, S], F32, AT_RA)]
+        scatter(dt2[0], l3, ra2[:, 0, :])
         zw = sb("zw", [P, S], U32)
         zs = sb("zs", [P, S], U8)
-        weave(nc.scalar.copy, zi[:], zc[:])
-        nc.vector.quantize_mx(out=zw[:].bitcast(FP8X4), scales=zs[:], in_=zi[:].rearrange("p c t -> p (c t)"))
+        quantise(zw[:], zs[:], zi[:])
+        rb2[0] = placed("rb2_0", [P, W], F32, AT_RB2_0)
+        make_rb2(0)
+        for t in range(2, PACK):
+            make_ra2(t)
+            make_rb2(t)
+        for t, offset in ((1, AT_DT3), (2, AT_DT2_2), (3, AT_DT2_3)):
+            dt2.append(placed("dt2_%d" % t, [P, S], F32, offset))
         for t in range(1, PACK):
-            dt2.append(reuse.tile([P, S], F32, name="dt2_%d" % t, align_bytes=64, offset=2048 * (t - 1)))
-        for t, which in ((1, 0), (2, 0), (1, 1), (3, 0), (2, 1), (3, 1)):
-            scatter_b(dt2[t], t, which)
+            scatter(dt2[t], l3, ra2[:, t, :])
+            scatter(dt2[t - 1], l4, rb2[t - 1][:])
+        scatter(dt2[PACK - 1], l4, rb2[PACK - 1][:])
 
-        z2c = reuse.tile([P, PACK, S], BF16, name="z2c", align_bytes=64, offset=6144)
-        npieces = len(PIECES)
+        def piece_tiles(name):
+            return [sb("%s_%d" % (name, k), [P, PACK, hi - lo], F32) for k, (lo, hi) in enumerate(PIECES)]
 
-        def piece_tiles(name, dtype=F32):
-            return [sb("%s_%d" % (name, k), [P, PACK, hi - lo], dtype) for k, (lo, hi) in enumerate(PIECES)]
+        def fetch_piece(dst, windows, lst, k):
+            for t in range(PACK):
+                scalar_gather(dst[k][:, t, :], windows[t], entries(lst, *PIECES[k]))
 
-        def piece_of(lst, k):
-            lo, hi = PIECES[k]
-            return lst[:, lo // 16:hi // 16]
-
+        z2p = sb("z2p", [P, 2, S, 2], BF16)
         a5, a6 = piece_tiles("a5"), piece_tiles("a6")
-
-        def round_z2(t):
-            nc.scalar.activation(z2c[:, t, :], dt2[t][:], ACT.Copy, scale=gain[:, t:t + 1])
-
-        def fetch_piece(dst, windows, lst, k, ts):
-            for t in ts:
-                gather_s(dst[k][:, t, :], windows[t], piece_of(lst, k))
-
-        round_z2(0)
+        for t in range(2):
+            gpsimd_round(z2p[:, 0, :, t], dt2[t], t)
         a = [sb("a%d" % t, [P, S], F32) for t in range(PACK)]
-        for t in range(PACK):
+        for h in range(2):
+            nc.scalar.copy(a[0][:, cols(h)], product("aacc0_%d" % h, w2w, w2s, 0, zw[:, cols(h)], zs[:, cols(h)])[:])
+        for t in range(1, PACK):
             nc.scalar.copy(a[t][:], product("aacc%d" % t, w2w, w2s, t, zw[:], zs[:])[:])
+        for k in range(len(PIECES)):
+            fetch_piece(a5, a, l5, k)
+            fetch_piece(a6, a, l6, k)
 
-        fetch_piece(a5, a, l5, 0, range(PACK))
-        round_z2(1)
-        fetch_piece(a6, a, l6, 0, range(2))
-        round_z2(2)
-        fetch_piece(a6, a, l6, 0, range(2, PACK))
-
-        nc.vector.tensor_scalar(z2c[:, 3, :], dt2[3][:], gain[:, 3:4], None, ALU.mult)
+        for t in range(2, PACK):
+            nc.vector.tensor_scalar(z2p[:, 1, :, t - 2], dt2[t][:], gain[:, t:t + 1], None, ALU.mult)
+        pair_words = z2p[:].rearrange("p u c e -> p u (c e)").bitcast(I32)
         z2i = [sb("z2i%d" % h, [P, HALF, PACK], BF16) for h in range(2)]
         z2w = sb("z2w", [P, S], U32)
         z2s = sb("z2s", [P, S], U8)
         for h in range(2):
-            weave(nc.vector.tensor_copy, z2i[h][:], z2c[:, :, cols(h)])
+            two_words = z2i[h][:].rearrange("p c t -> p (c t)").bitcast(I32).rearrange("p (c u) -> p c u", u=2)
+            interleave(nc.vector.tensor_copy, two_words, pair_words[:, :, cols(h)])
         for h in range(2):
-            nc.vector.quantize_mx(out=z2w[:, cols(h)].bitcast(FP8X4), scales=z2s[:, cols(h)],
-                                  in_=z2i[h][:].rearrange("p c t -> p (c t)"))
+            quantise(z2w[:, cols(h)], z2s[:, cols(h)], z2i[h][:])
         b = [sb("b%d" % t, [P, S], F32) for t in range(PACK)]
-        for h in range(2):
-            for t in range(PACK):
-                copy_out = nc.vector.tensor_copy if (h, t) in ((0, 2), (0, 3), (1, 0)) else nc.scalar.copy
-                copy_out(b[t][:, cols(h)], product("bacc%d_%d" % (t, h), w2w, w2s, t, z2w[:, cols(h)], z2s[:, cols(h)])[:])
+        for ts in (range(0, 2), range(2, PACK)):
+            for h, t in ((h, t) for h in range(2) for t in ts):
+                copy_out = nc.vector.tensor_copy if h + t == 1 else nc.scalar.copy
+                acc = product("bacc%d_%d" % (t, h), w2w, w2s, t, z2w[:, cols(h)], z2s[:, cols(h)])
+                copy_out(b[t][:, cols(h)], acc[:])
 
-        s1, s2, b7, b8, res = (piece_tiles(name) for name in ("s1", "s2", "b7", "b8", "res"))
-        oi = [sb("oi%d" % k, [P, hi - lo, PACK], BF16) for k, (lo, hi) in enumerate(PIECES)]
+        s1, s2, b8, res = (piece_tiles(name) for name in ("s1", "s2", "b8", "res"))
+        b7_last = sb("b7_last", [P, PACK, PIECES[1][1] - PIECES[1][0]], F32)
+        oi = [sb("oi%d" % j, [P, hi - lo, PACK], BF16) for j, (k, lo, hi) in enumerate(OUT_RANGES)]
         ow = sb("ow", [P, S], U32)
         osc = sb("osc", [P, S], U8)
         out0_rows = out_0.rearrange("(p t) c -> p t c", t=PACK)
         out1_words = words_of(out_1)
 
-        for k in range(npieces):
-            if k > 0:
-                fetch_piece(a5, a, l5, k, range(PACK))
-                fetch_piece(a6, a, l6, k, range(PACK))
-            fetch_piece(b8, b, l8, k, range(PACK))
-            fetch_piece(b7, b, l7, k, range(FUSED[k], PACK))
-        for k, (lo, hi) in enumerate(PIECES):
-            f = FUSED[k]
-            for t in range(f):
-                nc.vector.tensor_tensor(s1[k][:, t, :], b[t][:].indirect(piece_of(l7, k)), a5[k][:, t, :], ALU.add)
+        def sum_b8(k):
             nc.vector.tensor_tensor(s2[k][:], b8[k][:], a6[k][:], ALU.add)
-            if f < PACK:
-                nc.vector.tensor_tensor(s1[k][:, f:, :], b7[k][:, f:, :], a5[k][:, f:, :], ALU.add)
+
+        def join(k):
             nc.vector.tensor_tensor(res[k][:], s1[k][:], s2[k][:], ALU.max)
-            nc.sync.dma_start(out0_rows[:, :, lo:hi], res[k][:])
-            weave(nc.scalar.copy if k < npieces - 1 else nc.vector.tensor_copy, oi[k][:], res[k][:])
-        for k, (lo, hi) in enumerate(PIECES):
-            nc.vector.quantize_mx(out=ow[:, lo:hi].bitcast(FP8X4), scales=osc[:, lo:hi],
-                                  in_=oi[k][:].rearrange("p c t -> p (c t)"))
-            nc.sync.dma_start(out1_words[:, lo:hi], ow[:, lo:hi].bitcast(I32))
-        for q in range(4):
+            nc.sync.dma_start(out0_rows[:, :, slice(*PIECES[k])], res[k][:])
+
+        for k in range(len(PIECES)):
+            fetch_piece(b8, b, l8, k)
+        for t in range(PACK):
+            scalar_gather(b7_last[:, t, :], b[t], entries(l7, *PIECES[1]))
+        for t in range(PACK):
+            nc.vector.tensor_tensor(s1[0][:, t, :], b[t][:].indirect(entries(l7, *PIECES[0])), a5[0][:, t, :], ALU.add)
+        sum_b8(0)
+        join(0)
+        sum_b8(1)
+        nc.vector.tensor_tensor(s1[1][:], b7_last[:], a5[1][:], ALU.add)
+        join(1)
+
+        for j, (k, lo, hi) in enumerate(OUT_RANGES):
+            engine_copy = nc.scalar.copy if k == 0 else nc.vector.tensor_copy
+            interleave(engine_copy, oi[j][:], res[k][:, :, lo - PIECES[k][0]:hi - PIECES[k][0]])
+            quantise(ow[:, lo:hi], osc[:, lo:hi], oi[j][:])
+            if j == 0:
+                nc.sync.dma_start(out1_words[:, cols(0)], ow[:, cols(0)].bitcast(I32))
+        nc.sync.dma_start(out1_words[:, cols(1)], ow[:, cols(1)].bitcast(I32))
+        for q in range(QUADRANTS):
             queue = nc.sync if q % 2 else nc.scalar
-            queue.dma_start(out_2[0, 4 * q:4 * q + 4, :].bitcast(I32), osc[32 * q:32 * q + 4, :].bitcast(I32))
+            queue.dma_start(scale_rows(out_2, q), live_rows(osc, q))

from contextlib import ExitStack

import concourse.mybir as mybir

F32 = mybir.dt.float32
BF16 = mybir.dt.bfloat16
I32 = mybir.dt.int32
U32 = mybir.dt.uint32
U16 = mybir.dt.uint16
U8 = mybir.dt.uint8
FP8X4 = mybir.dt.float8_e4m3fn_x4
ALU = mybir.AluOpType
ACT = mybir.ActivationFunctionType

P = 128
PACK = 4
QUADRANTS = 4
T = 2048
S = 512
W = 256
HALF = S // 2
PER_COLUMN = 16

PIECES = ((0, 384), (384, 512))
OUT_RANGES = ((0, 0, 256), (1, 384, 512), (0, 256, 384))

AT_RA = 0
AT_DT3 = 5120
AT_ZI = 8192
AT_RB2_0 = AT_ZI - 512
AT_DT2_2 = AT_ZI + 512
AT_DT2_3 = AT_DT2_2 + 2048

FLOPS = 3 * 2 * 512 * 512 * 512


def tile_picked_tiepathborderduel_none_po_kernel(
    tc, x_words, x_scales, w1_words, w1_scales, gn, w2_words, w2_scales,
    offs, n1, n2, n3, n4, n5, n6, n7, n8, out_0, out_1, out_2,
):
    nc = tc.nc
    with ExitStack() as ctx:
        lists = ctx.enter_context(tc.tile_pool(name="lists", bufs=1))
        keep = ctx.enter_context(tc.tile_pool(name="keep", bufs=1))
        reuse = ctx.enter_context(tc.tile_pool(name="reuse", bufs=1))
        psum = ctx.enter_context(tc.psum_pool(name="psum", bufs=8))

        def sb(name, shape, dtype):
            return keep.tile(shape, dtype, name=name, tag=name, align_bytes=64)

        def placed(name, shape, dtype, offset):
            return reuse.tile(shape, dtype, name=name, align_bytes=64, offset=offset)

        def load_list(name, src):
            tile = lists.tile(list(src.shape), U16, name=name)
            nc.sync.dma_start(tile[:], src)
            return tile

        def entries(lst, lo, hi):
            return lst[:, lo // PER_COLUMN:hi // PER_COLUMN]

        def cols(h):
            return slice(h * HALF, (h + 1) * HALF)

        def words_of(dram):
            return dram[0].rearrange("p n t -> p (n t)").bitcast(I32)

        def scale_rows(dram, q):
            return dram[0, 4 * q:4 * q + 4, :].bitcast(I32)

        def live_rows(scales, q):
            return scales[32 * q:32 * q + 4, :].bitcast(I32)

        def dealt(ap):
            return ap.rearrange("p (m t) -> p t m", t=PACK)

        def product(name, ww, ws, t, words, scales):
            acc = psum.tile([P, words.shape[1]], F32, name=name, tag="acc")
            nc.tensor.matmul_mx(out=acc[:], lhsT=ww[:, t, :].bitcast(FP8X4), lhsT_scale=ws[:, t, :],
                                rhs=words.bitcast(FP8X4), rhs_scale=scales, start=True, stop=True)
            return acc

        def scalar_gather(out, window, offsets):
            nc.scalar.activation(out, window[:].indirect(offsets), ACT.Copy)

        def scatter(window, lst, values):
            nc.vector.tensor_copy(window[:].indirect(lst[:]), values)

        def interleave(engine_copy, dst, src):
            engine_copy(dst.rearrange("p (c i) t -> p c t i", i=4), src.rearrange("p t (c i) -> p c t i", i=4))

        def quantise(words, scales, interleaved):
            nc.vector.quantize_mx(out=words.bitcast(FP8X4), scales=scales,
                                  in_=interleaved.rearrange("p c t -> p (c t)"))

        xs = sb("xs", [P, T], U8)
        w1s_raw = sb("w1s_raw", [P, S], U8)
        w2s_raw = sb("w2s_raw", [P, S], U8)
        nc.vector.memset(xs[:].bitcast(I32), 0)
        nc.gpsimd.memset(w1s_raw[:].bitcast(I32), 0)
        nc.vector.memset(w2s_raw[:].bitcast(I32), 0)
        l_offs = load_list("l_offs", offs)
        l1 = load_list("l1", n1)
        l2 = load_list("l2", n2)
        xw = sb("xw", [P, T], U32)
        nc.sync.dma_start(xw[:].bitcast(I32), words_of(x_words))
        for q in range(QUADRANTS):
            nc.scalar.dma_start(live_rows(xs, q), scale_rows(x_scales, q))
        w1w_raw = sb("w1w_raw", [P, S], I32)
        nc.sync.dma_start(w1w_raw[:], words_of(w1_words))
        for q in range(QUADRANTS):
            queue = nc.scalar if q < QUADRANTS // 2 else nc.gpsimd
            queue.dma_start(live_rows(w1s_raw, q), scale_rows(w1_scales, q))
        w2w_raw = sb("w2w_raw", [P, S], I32)
        nc.sync.dma_start(w2w_raw[:], words_of(w2_words))
        l3 = load_list("l3", n3)
        l4 = load_list("l4", n4)
        gain = sb("gain", [P, PACK], F32)
        nc.sync.dma_start(gain[:], gn.rearrange("(p t) o -> p (t o)", t=PACK))
        for q in range(QUADRANTS):
            nc.sync.dma_start(live_rows(w2s_raw, q), scale_rows(w2_scales, q))
        l5 = load_list("l5", n5)
        l6 = load_list("l6", n6)
        l7 = load_list("l7", n7)
        l8 = load_list("l8", n8)

        xgs = sb("xgs", [P, S], U8)
        xg = sb("xg", [P, S], U32)
        w1s = sb("w1s", [P, PACK, P], U8)
        w1w = sb("w1w", [P, PACK, P], I32)
        nc.vector.tensor_copy(xgs[:], xs[:].indirect(l_offs[:]))
        nc.vector.tensor_copy(xg[:, cols(0)], xw[:].indirect(entries(l_offs, 0, HALF)))
        nc.gpsimd.tensor_copy(w1w[:, 0, :], dealt(w1w_raw[:])[:, 0, :])
        nc.gpsimd.tensor_copy(w1s[:, 0, :], dealt(w1s_raw[:])[:, 0, :])
        nc.vector.tensor_copy(xg[:, cols(1)], xw[:].indirect(entries(l_offs, HALF, S)))
        nc.vector.tensor_copy(w1w[:, 1:, :], dealt(w1w_raw[:])[:, 1:, :])
        nc.vector.tensor_copy(w1s[:, 1:, :], dealt(w1s_raw[:])[:, 1:, :])

        y = [sb("y%d" % t, [P, S], F32) for t in range(PACK)]
        y0_acc = [product("y0_%d" % h, w1w, w1s, 0, xg[:, cols(h)], xgs[:, cols(h)]) for h in range(2)]
        y_acc = {t: product("yacc%d" % t, w1w, w1s, t, xg[:], xgs[:]) for t in range(1, PACK)}

        w2s = sb("w2s", [P, PACK, P], U8)
        w2w = sb("w2w", [P, PACK, P], I32)

        pa = sb("pa", [P, PACK, W], F32)
        pb = sb("pb", [P, PACK, W], F32)
        ra = placed("ra", [P, PACK, W], F32, AT_RA)
        rb = sb("rb", [P, PACK, W], F32)
        pa2 = sb("pa2", [P, PACK, W], F32)
        pb2 = sb("pb2", [P, PACK, W], F32)
        diff0 = placed("diff0", [P, 1, W], F32, AT_ZI)
        diff123 = sb("diff123", [P, PACK - 1, W], F32)
        ra2 = sb("ra2", [P, PACK, W], F32)
        rb2 = {t: sb("rb2_%d" % t, [P, W], F32) for t in range(1, PACK)}
        sp = sb("sp", [P, PACK, W], F32)
        sn = sb("sn", [P, PACK, W], F32)
        dt = [sb("dt%d" % t, [P, S], F32) for t in range(PACK - 1)] + [placed("dt3", [P, S], F32, AT_DT3)]

        def larger(t0, t1):
            nc.vector.tensor_tensor(ra[:, t0:t1, :], pa[:, t0:t1, :], pb[:, t0:t1, :], ALU.max)

        def smaller(t0, t1):
            nc.vector.tensor_tensor(rb[:, t0:t1, :], pa[:, t0:t1, :], pb[:, t0:t1, :], ALU.min)

        def put_ra(t):
            scatter(dt[t], l1, ra[:, t, :])

        def put_rb(t):
            scatter(dt[t], l2, rb[:, t, :])

        def fetch_pa_pb(t):
            scalar_gather(pa[:, t, :], y[t], l1[:])
            scalar_gather(pb[:, t, :], y[t], l2[:])

        def fetch_pa2_pb2(t):
            scalar_gather(pa2[:, t, :], y[t], l3[:])
            scalar_gather(pb2[:, t, :], y[t], l4[:])

        def diff(t0, t1):
            return diff0[:] if t0 == 0 else diff123[:, t0 - 1:t1 - 1, :]

        def subtract(t):
            nc.gpsimd.tensor_tensor(diff(t, t + 1), pa2[:, t:t + 1, :], pb2[:, t:t + 1, :], ALU.subtract)

        def sigmoids(t0, t1):
            nc.scalar.activation(sp[:, t0:t1, :], diff(t0, t1), ACT.Sigmoid)
            nc.scalar.activation(sn[:, t0:t1, :], diff(t0, t1), ACT.Sigmoid, scale=-1.0)

        def make_ra2(t):
            nc.gpsimd.tensor_tensor(ra2[:, t, :], pa2[:, t, :], sp[:, t, :], ALU.mult)

        def make_rb2(t):
            nc.gpsimd.tensor_tensor(rb2[t][:], pb2[:, t, :], sn[:, t, :], ALU.mult)

        def gpsimd_round(out, window, t):
            nc.gpsimd.tensor_scalar(out, window[:], gain[:, t:t + 1], 0.0, ALU.mult, ALU.add)

        for h in range(2):
            nc.scalar.copy(y[0][:, cols(h)], y0_acc[h][:])
        nc.vector.tensor_copy(pa[:, 0, :], y[0][:].indirect(l1[:]))
        scalar_gather(pb[:, 0, :], y[0], l2[:])
        larger(0, 1)
        put_ra(0)
        nc.scalar.copy(y[1][:], y_acc[1][:])
        fetch_pa_pb(1)
        larger(1, 2)
        smaller(0, 2)
        put_ra(1)
        put_rb(0)
        put_rb(1)
        nc.scalar.copy(y[2][:], y_acc[2][:])
        fetch_pa2_pb2(0)
        subtract(0)
        nc.scalar.copy(y[3][:], y_acc[3][:])
        fetch_pa_pb(2)
        fetch_pa_pb(3)
        larger(2, 4)
        smaller(2, 4)
        for put in (put_ra, put_rb):
            put(2)
            put(3)

        fetch_pa2_pb2(1)
        subtract(1)
        sigmoids(0, 1)
        sigmoids(1, 2)
        make_ra2(0)
        zi = placed("zi", [P, S, PACK], BF16, AT_ZI)
        for t in range(2):
            gpsimd_round(zi[:, :, t], dt[t], t)
        make_ra2(1)
        make_rb2(1)
        for t in range(2, PACK):
            fetch_pa2_pb2(t)
            subtract(t)
        for t in range(PACK):
            nc.gpsimd.tensor_copy(w2w[:, t, :], dealt(w2w_raw[:])[:, t, :])
            nc.gpsimd.tensor_copy(w2s[:, t, :], dealt(w2s_raw[:])[:, t, :])
        for t in range(2, PACK):
            nc.scalar.activation(zi[:, :, t], dt[t][:], ACT.Copy, scale=gain[:, t:t + 1])
        sigmoids(2, 4)

        dt2 = [placed("dt2_0", [P, S], F32, AT_RA)]
        scatter(dt2[0], l3, ra2[:, 0, :])
        zw = sb("zw", [P, S], U32)
        zs = sb("zs", [P, S], U8)
        quantise(zw[:], zs[:], zi[:])
        rb2[0] = placed("rb2_0", [P, W], F32, AT_RB2_0)
        make_rb2(0)
        for t in range(2, PACK):
            make_ra2(t)
            make_rb2(t)
        for t, offset in ((1, AT_DT3), (2, AT_DT2_2), (3, AT_DT2_3)):
            dt2.append(placed("dt2_%d" % t, [P, S], F32, offset))
        for t in range(1, PACK):
            scatter(dt2[t], l3, ra2[:, t, :])
            scatter(dt2[t - 1], l4, rb2[t - 1][:])
        scatter(dt2[PACK - 1], l4, rb2[PACK - 1][:])

        def piece_tiles(name):
            return [sb("%s_%d" % (name, k), [P, PACK, hi - lo], F32) for k, (lo, hi) in enumerate(PIECES)]

        def fetch_piece(dst, windows, lst, k):
            for t in range(PACK):
                scalar_gather(dst[k][:, t, :], windows[t], entries(lst, *PIECES[k]))

        z2p = sb("z2p", [P, 2, S, 2], BF16)
        a5, a6 = piece_tiles("a5"), piece_tiles("a6")
        for t in range(2):
            gpsimd_round(z2p[:, 0, :, t], dt2[t], t)
        a = [sb("a%d" % t, [P, S], F32) for t in range(PACK)]
        for h in range(2):
            nc.scalar.copy(a[0][:, cols(h)], product("aacc0_%d" % h, w2w, w2s, 0, zw[:, cols(h)], zs[:, cols(h)])[:])
        for t in range(1, PACK):
            nc.scalar.copy(a[t][:], product("aacc%d" % t, w2w, w2s, t, zw[:], zs[:])[:])
        for k in range(len(PIECES)):
            fetch_piece(a5, a, l5, k)
            fetch_piece(a6, a, l6, k)

        for t in range(2, PACK):
            nc.vector.tensor_scalar(z2p[:, 1, :, t - 2], dt2[t][:], gain[:, t:t + 1], None, ALU.mult)
        pair_words = z2p[:].rearrange("p u c e -> p u (c e)").bitcast(I32)
        z2i = [sb("z2i%d" % h, [P, HALF, PACK], BF16) for h in range(2)]
        z2w = sb("z2w", [P, S], U32)
        z2s = sb("z2s", [P, S], U8)
        for h in range(2):
            two_words = z2i[h][:].rearrange("p c t -> p (c t)").bitcast(I32).rearrange("p (c u) -> p c u", u=2)
            interleave(nc.vector.tensor_copy, two_words, pair_words[:, :, cols(h)])
        for h in range(2):
            quantise(z2w[:, cols(h)], z2s[:, cols(h)], z2i[h][:])
        b = [sb("b%d" % t, [P, S], F32) for t in range(PACK)]
        for ts in (range(0, 2), range(2, PACK)):
            for h, t in ((h, t) for h in range(2) for t in ts):
                copy_out = nc.vector.tensor_copy if h + t == 1 else nc.scalar.copy
                acc = product("bacc%d_%d" % (t, h), w2w, w2s, t, z2w[:, cols(h)], z2s[:, cols(h)])
                copy_out(b[t][:, cols(h)], acc[:])

        s1, s2, b8, res = (piece_tiles(name) for name in ("s1", "s2", "b8", "res"))
        b7_last = sb("b7_last", [P, PACK, PIECES[1][1] - PIECES[1][0]], F32)
        oi = [sb("oi%d" % j, [P, hi - lo, PACK], BF16) for j, (k, lo, hi) in enumerate(OUT_RANGES)]
        ow = sb("ow", [P, S], U32)
        osc = sb("osc", [P, S], U8)
        out0_rows = out_0.rearrange("(p t) c -> p t c", t=PACK)
        out1_words = words_of(out_1)

        def sum_b8(k):
            nc.vector.tensor_tensor(s2[k][:], b8[k][:], a6[k][:], ALU.add)

        def join(k):
            nc.vector.tensor_tensor(res[k][:], s1[k][:], s2[k][:], ALU.max)
            nc.sync.dma_start(out0_rows[:, :, slice(*PIECES[k])], res[k][:])

        for k in range(len(PIECES)):
            fetch_piece(b8, b, l8, k)
        for t in range(PACK):
            scalar_gather(b7_last[:, t, :], b[t], entries(l7, *PIECES[1]))
        for t in range(PACK):
            nc.vector.tensor_tensor(s1[0][:, t, :], b[t][:].indirect(entries(l7, *PIECES[0])), a5[0][:, t, :], ALU.add)
        sum_b8(0)
        join(0)
        sum_b8(1)
        nc.vector.tensor_tensor(s1[1][:], b7_last[:], a5[1][:], ALU.add)
        join(1)

        for j, (k, lo, hi) in enumerate(OUT_RANGES):
            engine_copy = nc.scalar.copy if k == 0 else nc.vector.tensor_copy
            interleave(engine_copy, oi[j][:], res[k][:, :, lo - PIECES[k][0]:hi - PIECES[k][0]])
            quantise(ow[:, lo:hi], osc[:, lo:hi], oi[j][:])
            if j == 0:
                nc.sync.dma_start(out1_words[:, cols(0)], ow[:, cols(0)].bitcast(I32))
        nc.sync.dma_start(out1_words[:, cols(1)], ow[:, cols(1)].bitcast(I32))
        for q in range(QUADRANTS):
            queue = nc.sync if q % 2 else nc.scalar
            queue.dma_start(scale_rows(out_2, q), live_rows(osc, q))
